import numpy as np
import ml_dtypes


def mxq(x, axis, fmt="e4m3"):
    dtype, down = {"e4m3": (ml_dtypes.float8_e4m3fn, 7), "e5m2": (ml_dtypes.float8_e5m2, 14)}[fmt]
    v = np.moveaxis(np.asarray(x, np.float32).astype(ml_dtypes.bfloat16).astype(np.float64), axis, -1)
    blocks = v.reshape(v.shape[:-1] + (-1, 32))
    amax = np.abs(blocks).max(-1, keepdims=True)
    byte = np.maximum(np.where(amax > 0, np.frexp(amax)[1] - 1 + 127, 0) - down, 1)
    scale = np.exp2(byte - 127.0)
    codes = (blocks / scale).astype(np.float32).astype(dtype).astype(np.float64)
    return np.moveaxis((codes * scale).reshape(v.shape), -1, axis)


WIDE = False


def mx_kscale(k):
    if not WIDE:
        return np.ones(k)
    levels = np.array([10, -10, 5, -5, 0])
    if k % 512:
        return np.exp2(np.random.permutation(np.resize(levels, k // 32))).repeat(32)
    a = np.empty((k // 512, 16))
    for p in range(k // 512):
        a[p, :8] = np.random.permutation(np.resize(levels, 8))
        for g in range(8):
            far = levels[np.abs(levels - a[p, g]) >= 10]
            a[p, g + 8] = far[np.random.randint(len(far))]
    return np.exp2(a.ravel()).repeat(32)


def f64(x):
    return np.asarray(x).astype(np.float64)


def striped(idx):
    return np.tile(idx.reshape(-1, 16).T, (8, 1)).astype(np.uint16)


def unstriped(offs):
    return offs[:16].T.reshape(-1).astype(np.int64)


def pack_weight(w):
    k, n = w.shape
    w = f64(np.asarray(w, np.float32).astype(ml_dtypes.bfloat16)).reshape(k // 32, 32, n)
    amax = np.abs(w).max(1)
    byte = np.clip(np.where(amax > 0, np.frexp(amax)[1] - 1 + 127 - 7, 1), 1, 254)
    scaled = (w * np.exp2(127.0 - byte)[:, None, :]).reshape(k, n).astype(np.float32)
    words = np.ascontiguousarray(scaled.reshape(k // 512, 128, 4, n).transpose(0, 1, 3, 2)).astype(ml_dtypes.float8_e4m3fn).view(np.uint8)
    return words, np.ascontiguousarray(byte.astype(np.uint8).reshape(k // 512, 16, n))


def unpack_weight(words, scales):
    g, p, n, _ = words.shape
    vals = np.ascontiguousarray(words).view(ml_dtypes.float8_e4m3fn).astype(np.float64) * np.repeat(np.exp2(scales.astype(np.float64) - 127.0), 8, axis=1)[..., None]
    return vals.transpose(0, 1, 3, 2).reshape(g * 512, n)


def gelu(v):
    return 0.5 * v * (1.0 + np.tanh(np.sqrt(2.0 / np.pi) * (v + 0.044715 * v**3)))


K, T, N, U = 512, 1024, 128, 2048
P = 2 ** 7


def setup_inputs():
    n = np.random.standard_normal
    s = mx_kscale(K)[:, None]
    packed_xT = pack_weight(n((K, T)) * s)
    return {
        "x_words": packed_xT[0],
        "x_scales": packed_xT[1],
        "gate": np.tile(np.random.uniform(0.5, 1.5, T), (P, 1)).astype(np.float32),
        "w1": (n((K, N)) / np.sqrt(K) / s).astype(np.float32),
        "dst": striped(np.random.permutation(U)[:T]),
    }


def reference(x_words, x_scales, gate, w1, dst):
    xq = unpack_weight(x_words, x_scales)
    y = gelu(mxq(f64(w1), 0, "e4m3").T @ xq)
    out = np.zeros((N, U))
    out[:, unstriped(dst)] = y * f64(gate)[:1]
    return out

@@ -1,0 +1,81 @@
+from contextlib import ExitStack
+
+import concourse.mybir as mybir
+
+K, T, N, U = 512, 1024, 128, 2048
+FLOPS = 2 * K * T * N
+
+F32 = mybir.dt.float32
+BF16 = mybir.dt.bfloat16
+I32 = mybir.dt.int32
+U32 = mybir.dt.uint32
+U16 = mybir.dt.uint16
+U8 = mybir.dt.uint8
+FP8X4 = mybir.dt.float8_e4m3fn_x4
+GELU = mybir.ActivationFunctionType.Gelu_apprx_tanh
+MULT = mybir.AluOpType.mult
+
+P = 128
+PACK = 4
+HEAD = 256
+
+
+def tile_picked_wroute2_lingelu_l_kernel(tc, x_words, x_scales, gate, w1, dst, out):
+    nc = tc.nc
+    with ExitStack() as ctx:
+        keep = ctx.enter_context(tc.tile_pool(name="keep", bufs=1))
+        psum = ctx.enter_context(tc.psum_pool(name="psum", bufs=1))
+
+        offsets = keep.tile([P, T // 16], U16, name="offsets")
+        w_raw = keep.tile([P, PACK, N], F32, name="w_raw")
+        w_grouped = keep.tile([P, N, PACK], BF16, name="w_grouped", align_bytes=64)
+        w_codes = keep.tile([P, N], U32, name="w_codes", align_bytes=64)
+        w_plane = keep.tile([P, N], U8, name="w_plane", align_bytes=64)
+        x_plane = keep.tile([P, T], U8, name="x_plane", align_bytes=64)
+        x_head = keep.tile([P, HEAD], U32, name="x_head", align_bytes=64)
+        x_rest = keep.tile([P, T - HEAD], U32, name="x_rest", align_bytes=64)
+        g_head = keep.tile([P, HEAD], F32, name="g_head")
+        g_rest = keep.tile([P, T - HEAD], F32, name="g_rest")
+        y_head = keep.tile([P, HEAD], F32, name="y_head")
+        y_rest = keep.tile([P, T - HEAD], F32, name="y_rest")
+        window = keep.tile([P, U], F32, name="window")
+        warm_in = keep.tile([P, 8], F32, name="warm_in")
+        warm_out = keep.tile([P, 8], F32, name="warm_out")
+
+        words = x_words[0].rearrange("p n t -> p (n t)")
+        nc.sync.dma_start(out=w_raw[:], in_=w1.rearrange("(p j) n -> p j n", j=PACK))
+        for q in range(4):
+            nc.scalar.dma_start(out=x_plane[32 * q : 32 * q + 4, :].bitcast(I32), in_=x_scales[0, 4 * q : 4 * q + 4, :].bitcast(I32))
+        nc.sync.dma_start(out=x_head[:].bitcast(I32), in_=words[:, : PACK * HEAD].bitcast(I32))
+        nc.sync.dma_start(out=x_rest[:].bitcast(I32), in_=words[:, PACK * HEAD :].bitcast(I32))
+        nc.sync.dma_start(out=g_head[:], in_=gate[:, :HEAD])
+        nc.sync.dma_start(offsets[:], dst)
+        nc.sync.dma_start(out=g_rest[:], in_=gate[:, HEAD:])
+
+        nc.vector.memset(warm_in[:], 0.0)
+        nc.scalar.activation(warm_out[:], warm_in[:], GELU)
+        nc.vector.memset(window[:], 0.0)
+
+        nc.vector.tensor_copy(
+            out=w_grouped[:].rearrange("p (c i) t -> p c t i", i=4),
+            in_=w_raw[:].rearrange("p t (c i) -> p c t i", i=4),
+        )
+        nc.vector.quantize_mx(out=w_codes[:].bitcast(FP8X4), scales=w_plane[:], in_=w_grouped[:].rearrange("p n t -> p (n t)"))
+
+        pieces = ((x_head, y_head, 0, 0, 256), (x_rest, y_rest, 0, 256, 256), (x_rest, y_rest, 256, 512, 512))
+        for i, (x_t, y_t, a, c, n) in enumerate(pieces):
+            acc = psum.tile([P, n], F32, name="acc%d" % i)
+            nc.tensor.matmul_mx(
+                out=acc[:],
+                lhsT=w_codes[:].bitcast(FP8X4),
+                lhsT_scale=w_plane[:],
+                rhs=x_t[:, a : a + n].bitcast(FP8X4),
+                rhs_scale=x_plane[:, c : c + n],
+                start=True,
+                stop=True,
+            )
+            nc.scalar.activation(y_t[:, a : a + n], acc[:], GELU)
+
+        nc.vector.tensor_tensor(window[:].indirect(offsets[:, : HEAD // 16]), y_head[:], g_head[:], MULT)
+        nc.vector.tensor_tensor(window[:].indirect(offsets[:, HEAD // 16 :]), y_rest[:], g_rest[:], MULT)
+        nc.sync.dma_start(out=out, in_=window[:])

@@ -18,6 +18,7 @@ MULT = mybir.AluOpType.mult
 P = 128
 PACK = 4
 HEAD = 256
+QT = 256
 
 
 def tile_picked_wroute2_lingelu_l_kernel(tc, x_words, x_scales, gate, w1, dst, out):
@@ -31,7 +32,7 @@ def tile_picked_wroute2_lingelu_l_kernel(tc, x_words, x_scales, gate, w1, dst, o
         w_grouped = keep.tile([P, N, PACK], BF16, name="w_grouped", align_bytes=64)
         w_codes = keep.tile([P, N], U32, name="w_codes", align_bytes=64)
         w_plane = keep.tile([P, N], U8, name="w_plane", align_bytes=64)
-        x_plane = keep.tile([P, T], U8, name="x_plane", align_bytes=64)
+        x_plane = keep.tile([P, QT], U8, name="x_plane", align_bytes=64)
         x_head = keep.tile([P, HEAD], U32, name="x_head", align_bytes=64)
         x_rest = keep.tile([P, T - HEAD], U32, name="x_rest", align_bytes=64)
         g_head = keep.tile([P, HEAD], F32, name="g_head")
@@ -43,12 +44,14 @@ def tile_picked_wroute2_lingelu_l_kernel(tc, x_words, x_scales, gate, w1, dst, o
         warm_out = keep.tile([P, 8], F32, name="warm_out")
 
         words = x_words[0].rearrange("p n t -> p (n t)")
+        nc.scalar.dma_start(out=x_plane[0 : 16, :].bitcast(I32), in_=x_scales[0, 0 : 4, :].bitcast(I32).rearrange("r (c n) -> c r n", c=4))
         nc.sync.dma_start(out=w_raw[:], in_=w1.rearrange("(p j) n -> p j n", j=PACK))
-        for q in range(4):
-            nc.scalar.dma_start(out=x_plane[32 * q : 32 * q + 4, :].bitcast(I32), in_=x_scales[0, 4 * q : 4 * q + 4, :].bitcast(I32))
         nc.sync.dma_start(out=x_head[:].bitcast(I32), in_=words[:, : PACK * HEAD].bitcast(I32))
-        nc.sync.dma_start(out=x_rest[:].bitcast(I32), in_=words[:, PACK * HEAD :].bitcast(I32))
+        nc.sync.dma_start(out=x_plane[32 : 48, :].bitcast(I32), in_=x_scales[0, 4 : 8, :].bitcast(I32).rearrange("r (c n) -> c r n", c=4))
+        nc.sync.dma_start(out=x_plane[64 : 80, :].bitcast(I32), in_=x_scales[0, 8 : 12, :].bitcast(I32).rearrange("r (c n) -> c r n", c=4))
+        nc.sync.dma_start(out=x_plane[96 : 112, :].bitcast(I32), in_=x_scales[0, 12 : 16, :].bitcast(I32).rearrange("r (c n) -> c r n", c=4))
         nc.sync.dma_start(out=g_head[:], in_=gate[:, :HEAD])
+        nc.sync.dma_start(out=x_rest[:].bitcast(I32), in_=words[:, PACK * HEAD :].bitcast(I32))
         nc.sync.dma_start(offsets[:], dst)
         nc.sync.dma_start(out=g_rest[:], in_=gate[:, HEAD:])
 
@@ -57,20 +60,25 @@ def tile_picked_wroute2_lingelu_l_kernel(tc, x_words, x_scales, gate, w1, dst, o
         nc.vector.memset(window[:], 0.0)
 
         nc.vector.tensor_copy(
-            out=w_grouped[:].rearrange("p (c i) t -> p c t i", i=4),
-            in_=w_raw[:].rearrange("p t (c i) -> p c t i", i=4),
+            out=w_grouped[:, :96, :].rearrange("p (c i) t -> p c t i", i=4),
+            in_=w_raw[:, :, :96].rearrange("p t (c i) -> p c t i", i=4),
+        )
+        nc.scalar.copy(
+            out=w_grouped[:, 96:, :].rearrange("p (c i) t -> p c t i", i=4),
+            in_=w_raw[:, :, 96:].rearrange("p t (c i) -> p c t i", i=4),
         )
         nc.vector.quantize_mx(out=w_codes[:].bitcast(FP8X4), scales=w_plane[:], in_=w_grouped[:].rearrange("p n t -> p (n t)"))
 
-        pieces = ((x_head, y_head, 0, 0, 256), (x_rest, y_rest, 0, 256, 256), (x_rest, y_rest, 256, 512, 512))
-        for i, (x_t, y_t, a, c, n) in enumerate(pieces):
+        pieces = ((0, 128), (128, 128), (256, 256), (512, 256), (768, 256))
+        for i, (c, n) in enumerate(pieces):
+            x_t, y_t, a = (x_head, y_head, c) if c < HEAD else (x_rest, y_rest, c - HEAD)
             acc = psum.tile([P, n], F32, name="acc%d" % i)
             nc.tensor.matmul_mx(
                 out=acc[:],
                 lhsT=w_codes[:].bitcast(FP8X4),
                 lhsT_scale=w_plane[:],
                 rhs=x_t[:, a : a + n].bitcast(FP8X4),
-                rhs_scale=x_plane[:, c : c + n],
+                rhs_scale=x_plane[4 * (c // QT) :, c % QT : c % QT + n],
                 start=True,
                 stop=True,
             )

@@ -19,6 +19,7 @@ P = 128
 PACK = 4
 HEAD = 256
 QT = 256
+XH = 512
 
 
 def tile_picked_wroute2_lingelu_l_kernel(tc, x_words, x_scales, gate, w1, dst, out):
@@ -33,8 +34,8 @@ def tile_picked_wroute2_lingelu_l_kernel(tc, x_words, x_scales, gate, w1, dst, o
         w_codes = keep.tile([P, N], U32, name="w_codes", align_bytes=64)
         w_plane = keep.tile([P, N], U8, name="w_plane", align_bytes=64)
         x_plane = keep.tile([P, QT], U8, name="x_plane", align_bytes=64)
-        x_head = keep.tile([P, HEAD], U32, name="x_head", align_bytes=64)
-        x_rest = keep.tile([P, T - HEAD], U32, name="x_rest", align_bytes=64)
+        x_head = keep.tile([P, XH], U32, name="x_head", align_bytes=64)
+        x_rest = keep.tile([P, T - XH], U32, name="x_rest", align_bytes=64)
         g_head = keep.tile([P, HEAD], F32, name="g_head")
         g_rest = keep.tile([P, T - HEAD], F32, name="g_rest")
         y_head = keep.tile([P, HEAD], F32, name="y_head")
@@ -46,38 +47,41 @@ def tile_picked_wroute2_lingelu_l_kernel(tc, x_words, x_scales, gate, w1, dst, o
         words = x_words[0].rearrange("p n t -> p (n t)")
         nc.scalar.dma_start(out=x_plane[0 : 16, :].bitcast(I32), in_=x_scales[0, 0 : 4, :].bitcast(I32).rearrange("r (c n) -> c r n", c=4))
         nc.sync.dma_start(out=w_raw[:], in_=w1.rearrange("(p j) n -> p j n", j=PACK))
-        nc.sync.dma_start(out=x_head[:].bitcast(I32), in_=words[:, : PACK * HEAD].bitcast(I32))
+        nc.sync.dma_start(out=x_head[:].bitcast(I32), in_=words[:, : PACK * XH].bitcast(I32))
         nc.sync.dma_start(out=x_plane[32 : 48, :].bitcast(I32), in_=x_scales[0, 4 : 8, :].bitcast(I32).rearrange("r (c n) -> c r n", c=4))
         nc.sync.dma_start(out=x_plane[64 : 80, :].bitcast(I32), in_=x_scales[0, 8 : 12, :].bitcast(I32).rearrange("r (c n) -> c r n", c=4))
         nc.sync.dma_start(out=x_plane[96 : 112, :].bitcast(I32), in_=x_scales[0, 12 : 16, :].bitcast(I32).rearrange("r (c n) -> c r n", c=4))
-        nc.sync.dma_start(out=g_head[:], in_=gate[:, :HEAD])
-        nc.sync.dma_start(out=x_rest[:].bitcast(I32), in_=words[:, PACK * HEAD :].bitcast(I32))
         nc.sync.dma_start(offsets[:], dst)
+        nc.sync.dma_start(out=g_head[:], in_=gate[:, :HEAD])
+        nc.sync.dma_start(out=x_rest[:].bitcast(I32), in_=words[:, PACK * XH :].bitcast(I32))
         nc.sync.dma_start(out=g_rest[:], in_=gate[:, HEAD:])
 
         nc.vector.memset(warm_in[:], 0.0)
         nc.scalar.activation(warm_out[:], warm_in[:], GELU)
         nc.vector.memset(window[:], 0.0)
 
-        nc.vector.tensor_copy(
-            out=w_grouped[:, :96, :].rearrange("p (c i) t -> p c t i", i=4),
-            in_=w_raw[:, :, :96].rearrange("p t (c i) -> p c t i", i=4),
-        )
-        nc.scalar.copy(
-            out=w_grouped[:, 96:, :].rearrange("p (c i) t -> p c t i", i=4),
-            in_=w_raw[:, :, 96:].rearrange("p t (c i) -> p c t i", i=4),
-        )
-        nc.vector.quantize_mx(out=w_codes[:].bitcast(FP8X4), scales=w_plane[:], in_=w_grouped[:].rearrange("p n t -> p (n t)"))
+        for lo, hi, cast in ((0, 64, nc.vector.tensor_copy), (64, 96, nc.vector.tensor_copy), (96, 128, nc.scalar.copy)):
+            cast(
+                out=w_grouped[:, lo:hi, :].rearrange("p (c i) t -> p c t i", i=4),
+                in_=w_raw[:, :, lo:hi].rearrange("p t (c i) -> p c t i", i=4),
+            )
+        for lo in (0, 64):
+            nc.vector.quantize_mx(
+                out=w_codes[:, lo : lo + 64].bitcast(FP8X4),
+                scales=w_plane[:, lo : lo + 64],
+                in_=w_grouped[:, lo : lo + 64, :].rearrange("p n t -> p (n t)"),
+            )
 
-        pieces = ((0, 128), (128, 128), (256, 256), (512, 256), (768, 256))
+        pieces = ((0, 128), (128, 128), (256, 256), (512, 128), (640, 128), (768, 256))
         for i, (c, n) in enumerate(pieces):
-            x_t, y_t, a = (x_head, y_head, c) if c < HEAD else (x_rest, y_rest, c - HEAD)
+            y_t, a = (y_head, c) if c < HEAD else (y_rest, c - HEAD)
+            x_t, b = (x_head, c) if c < XH else (x_rest, c - XH)
             acc = psum.tile([P, n], F32, name="acc%d" % i)
             nc.tensor.matmul_mx(
                 out=acc[:],
                 lhsT=w_codes[:].bitcast(FP8X4),
                 lhsT_scale=w_plane[:],
-                rhs=x_t[:, a : a + n].bitcast(FP8X4),
+                rhs=x_t[:, b : b + n].bitcast(FP8X4),
                 rhs_scale=x_plane[4 * (c // QT) :, c % QT : c % QT + n],
                 start=True,
                 stop=True,

@@ -45,12 +45,13 @@ def tile_picked_wroute2_lingelu_l_kernel(tc, x_words, x_scales, gate, w1, dst, o
         warm_out = keep.tile([P, 8], F32, name="warm_out")
 
         words = x_words[0].rearrange("p n t -> p (n t)")
-        nc.scalar.dma_start(out=x_plane[0 : 16, :].bitcast(I32), in_=x_scales[0, 0 : 4, :].bitcast(I32).rearrange("r (c n) -> c r n", c=4))
         nc.sync.dma_start(out=w_raw[:], in_=w1.rearrange("(p j) n -> p j n", j=PACK))
+        for q in range(4):
+            nc.sync.dma_start(
+                out=x_plane[32 * q : 32 * q + 16, :].bitcast(I32),
+                in_=x_scales[0, 4 * q : 4 * q + 4, :].bitcast(I32).rearrange("r (c n) -> c r n", c=4),
+            )
         nc.sync.dma_start(out=x_head[:].bitcast(I32), in_=words[:, : PACK * XH].bitcast(I32))
-        nc.sync.dma_start(out=x_plane[32 : 48, :].bitcast(I32), in_=x_scales[0, 4 : 8, :].bitcast(I32).rearrange("r (c n) -> c r n", c=4))
-        nc.sync.dma_start(out=x_plane[64 : 80, :].bitcast(I32), in_=x_scales[0, 8 : 12, :].bitcast(I32).rearrange("r (c n) -> c r n", c=4))
-        nc.sync.dma_start(out=x_plane[96 : 112, :].bitcast(I32), in_=x_scales[0, 12 : 16, :].bitcast(I32).rearrange("r (c n) -> c r n", c=4))
         nc.sync.dma_start(offsets[:], dst)
         nc.sync.dma_start(out=g_head[:], in_=gate[:, :HEAD])
         nc.sync.dma_start(out=x_rest[:].bitcast(I32), in_=words[:, PACK * XH :].bitcast(I32))
@@ -58,7 +59,7 @@ def tile_picked_wroute2_lingelu_l_kernel(tc, x_words, x_scales, gate, w1, dst, o
 
         nc.vector.memset(warm_in[:], 0.0)
         nc.scalar.activation(warm_out[:], warm_in[:], GELU)
-        nc.vector.memset(window[:], 0.0)
+        nc.vector.memset(window[:].bitcast(I32), 0)
 
         for lo, hi, cast in ((0, 64, nc.vector.tensor_copy), (64, 96, nc.vector.tensor_copy), (96, 128, nc.scalar.copy)):
             cast(

@@ -41,8 +41,6 @@ def tile_picked_wroute2_lingelu_l_kernel(tc, x_words, x_scales, gate, w1, dst, o
         y_head = keep.tile([P, HEAD], F32, name="y_head")
         y_rest = keep.tile([P, T - HEAD], F32, name="y_rest")
         window = keep.tile([P, U], F32, name="window")
-        warm_in = keep.tile([P, 8], F32, name="warm_in")
-        warm_out = keep.tile([P, 8], F32, name="warm_out")
 
         words = x_words[0].rearrange("p n t -> p (n t)")
         nc.sync.dma_start(out=w_raw[:], in_=w1.rearrange("(p j) n -> p j n", j=PACK))
@@ -57,11 +55,9 @@ def tile_picked_wroute2_lingelu_l_kernel(tc, x_words, x_scales, gate, w1, dst, o
         nc.sync.dma_start(out=x_rest[:].bitcast(I32), in_=words[:, PACK * XH :].bitcast(I32))
         nc.sync.dma_start(out=g_rest[:], in_=gate[:, HEAD:])
 
-        nc.vector.memset(warm_in[:], 0.0)
-        nc.scalar.activation(warm_out[:], warm_in[:], GELU)
         nc.vector.memset(window[:].bitcast(I32), 0)
 
-        for lo, hi, cast in ((0, 64, nc.vector.tensor_copy), (64, 96, nc.vector.tensor_copy), (96, 128, nc.scalar.copy)):
+        for lo, hi, cast in ((0, 64, nc.vector.tensor_copy), (64, 128, nc.vector.tensor_copy)):
             cast(
                 out=w_grouped[:, lo:hi, :].rearrange("p (c i) t -> p c t i", i=4),
                 in_=w_raw[:, :, lo:hi].rearrange("p t (c i) -> p c t i", i=4),

@@ -29,7 +29,7 @@ def tile_picked_wroute2_lingelu_l_kernel(tc, x_words, x_scales, gate, w1, dst, o
         psum = ctx.enter_context(tc.psum_pool(name="psum", bufs=1))
 
         offsets = keep.tile([P, T // 16], U16, name="offsets")
-        w_raw = keep.tile([P, PACK, N], F32, name="w_raw")
+        w_pairs = [keep.tile([P, 2, N], F32, name="w_pair%d" % h) for h in range(2)]
         w_grouped = keep.tile([P, N, PACK], BF16, name="w_grouped", align_bytes=64)
         w_codes = keep.tile([P, N], U32, name="w_codes", align_bytes=64)
         w_plane = keep.tile([P, N], U8, name="w_plane", align_bytes=64)
@@ -43,7 +43,8 @@ def tile_picked_wroute2_lingelu_l_kernel(tc, x_words, x_scales, gate, w1, dst, o
         window = keep.tile([P, U], F32, name="window")
 
         words = x_words[0].rearrange("p n t -> p (n t)")
-        nc.sync.dma_start(out=w_raw[:], in_=w1.rearrange("(p j) n -> p j n", j=PACK))
+        for h in range(2):
+            nc.sync.dma_start(out=w_pairs[h][:], in_=w1.rearrange("(p j) n -> p j n", j=PACK)[:, 2 * h : 2 * h + 2, :])
         for q in range(4):
             nc.sync.dma_start(
                 out=x_plane[32 * q : 32 * q + 16, :].bitcast(I32),
@@ -57,10 +58,10 @@ def tile_picked_wroute2_lingelu_l_kernel(tc, x_words, x_scales, gate, w1, dst, o
 
         nc.vector.memset(window[:].bitcast(I32), 0)
 
-        for lo, hi, cast in ((0, 64, nc.vector.tensor_copy), (64, 128, nc.vector.tensor_copy)):
-            cast(
-                out=w_grouped[:, lo:hi, :].rearrange("p (c i) t -> p c t i", i=4),
-                in_=w_raw[:, :, lo:hi].rearrange("p t (c i) -> p c t i", i=4),
+        for h, lo, hi in ((0, 0, 128), (1, 0, 64), (1, 64, 128)):
+            nc.vector.tensor_copy(
+                out=w_grouped[:, lo:hi, 2 * h : 2 * h + 2].rearrange("p (c i) t -> p c t i", i=4),
+                in_=w_pairs[h][:, :, lo:hi].rearrange("p t (c i) -> p c t i", i=4),
             )
         for lo in (0, 64):
             nc.vector.quantize_mx(

@@ -45,14 +45,14 @@ def tile_picked_wroute2_lingelu_l_kernel(tc, x_words, x_scales, gate, w1, dst, o
         words = x_words[0].rearrange("p n t -> p (n t)")
         for h in range(2):
             nc.sync.dma_start(out=w_pairs[h][:], in_=w1.rearrange("(p j) n -> p j n", j=PACK)[:, 2 * h : 2 * h + 2, :])
+        nc.sync.dma_start(out=x_head[:].bitcast(I32), in_=words[:, : PACK * XH].bitcast(I32))
         for q in range(4):
             nc.sync.dma_start(
                 out=x_plane[32 * q : 32 * q + 16, :].bitcast(I32),
                 in_=x_scales[0, 4 * q : 4 * q + 4, :].bitcast(I32).rearrange("r (c n) -> c r n", c=4),
             )
-        nc.sync.dma_start(out=x_head[:].bitcast(I32), in_=words[:, : PACK * XH].bitcast(I32))
-        nc.sync.dma_start(offsets[:], dst)
         nc.sync.dma_start(out=g_head[:], in_=gate[:, :HEAD])
+        nc.sync.dma_start(offsets[:], dst)
         nc.sync.dma_start(out=x_rest[:].bitcast(I32), in_=words[:, PACK * XH :].bitcast(I32))
         nc.sync.dma_start(out=g_rest[:], in_=gate[:, HEAD:])
 

@@ -19,7 +19,9 @@ P = 128
 PACK = 4
 HEAD = 256
 QT = 256
-XH = 512
+X_CUTS = (0, 256, 512, 768, 1024)
+G_CUTS = (256, 512, 768, 1024)
+PASSES = ((0, 128), (128, 128), (256, 256), (512, 256), (768, 256))
 
 
 def tile_picked_wroute2_lingelu_l_kernel(tc, x_words, x_scales, gate, w1, dst, out):
@@ -34,8 +36,7 @@ def tile_picked_wroute2_lingelu_l_kernel(tc, x_words, x_scales, gate, w1, dst, o
         w_codes = keep.tile([P, N], U32, name="w_codes", align_bytes=64)
         w_plane = keep.tile([P, N], U8, name="w_plane", align_bytes=64)
         x_plane = keep.tile([P, QT], U8, name="x_plane", align_bytes=64)
-        x_head = keep.tile([P, XH], U32, name="x_head", align_bytes=64)
-        x_rest = keep.tile([P, T - XH], U32, name="x_rest", align_bytes=64)
+        x_codes = keep.tile([P, T], U32, name="x_codes", align_bytes=64)
         g_head = keep.tile([P, HEAD], F32, name="g_head")
         g_rest = keep.tile([P, T - HEAD], F32, name="g_rest")
         y_head = keep.tile([P, HEAD], F32, name="y_head")
@@ -43,9 +44,13 @@ def tile_picked_wroute2_lingelu_l_kernel(tc, x_words, x_scales, gate, w1, dst, o
         window = keep.tile([P, U], F32, name="window")
 
         words = x_words[0].rearrange("p n t -> p (n t)")
+
+        def load_tokens(lo, hi):
+            nc.sync.dma_start(out=x_codes[:, lo:hi].bitcast(I32), in_=words[:, PACK * lo : PACK * hi].bitcast(I32))
+
         for h in range(2):
             nc.sync.dma_start(out=w_pairs[h][:], in_=w1.rearrange("(p j) n -> p j n", j=PACK)[:, 2 * h : 2 * h + 2, :])
-        nc.sync.dma_start(out=x_head[:].bitcast(I32), in_=words[:, : PACK * XH].bitcast(I32))
+        load_tokens(X_CUTS[0], X_CUTS[1])
         for q in range(4):
             nc.sync.dma_start(
                 out=x_plane[32 * q : 32 * q + 16, :].bitcast(I32),
@@ -53,8 +58,10 @@ def tile_picked_wroute2_lingelu_l_kernel(tc, x_words, x_scales, gate, w1, dst, o
             )
         nc.sync.dma_start(out=g_head[:], in_=gate[:, :HEAD])
         nc.sync.dma_start(offsets[:], dst)
-        nc.sync.dma_start(out=x_rest[:].bitcast(I32), in_=words[:, PACK * XH :].bitcast(I32))
-        nc.sync.dma_start(out=g_rest[:], in_=gate[:, HEAD:])
+        for lo, hi in zip(X_CUTS[1:-1], X_CUTS[2:]):
+            load_tokens(lo, hi)
+        for lo, hi in zip(G_CUTS[:-1], G_CUTS[1:]):
+            nc.sync.dma_start(out=g_rest[:, lo - HEAD : hi - HEAD], in_=gate[:, lo:hi])
 
         nc.vector.memset(window[:].bitcast(I32), 0)
 
@@ -70,16 +77,14 @@ def tile_picked_wroute2_lingelu_l_kernel(tc, x_words, x_scales, gate, w1, dst, o
                 in_=w_grouped[:, lo : lo + 64, :].rearrange("p n t -> p (n t)"),
             )
 
-        pieces = ((0, 128), (128, 128), (256, 256), (512, 128), (640, 128), (768, 256))
-        for i, (c, n) in enumerate(pieces):
+        for i, (c, n) in enumerate(PASSES):
             y_t, a = (y_head, c) if c < HEAD else (y_rest, c - HEAD)
-            x_t, b = (x_head, c) if c < XH else (x_rest, c - XH)
             acc = psum.tile([P, n], F32, name="acc%d" % i)
             nc.tensor.matmul_mx(
                 out=acc[:],
                 lhsT=w_codes[:].bitcast(FP8X4),
                 lhsT_scale=w_plane[:],
-                rhs=x_t[:, b : b + n].bitcast(FP8X4),
+                rhs=x_codes[:, c : c + n].bitcast(FP8X4),
                 rhs_scale=x_plane[4 * (c // QT) :, c % QT : c % QT + n],
                 start=True,
                 stop=True,

@@ -67,8 +67,8 @@ def tile_picked_wroute2_lingelu_l_kernel(tc, x_words, x_scales, gate, w1, dst, o
 
         for h, lo, hi in ((0, 0, 128), (1, 0, 64), (1, 64, 128)):
             nc.vector.tensor_copy(
-                out=w_grouped[:, lo:hi, 2 * h : 2 * h + 2].rearrange("p (c i) t -> p c t i", i=4),
-                in_=w_pairs[h][:, :, lo:hi].rearrange("p t (c i) -> p c t i", i=4),
+                out=w_grouped[:, lo:hi, 2 * h : 2 * h + 2],
+                in_=w_pairs[h][:, :, lo:hi].rearrange("p t n -> p n t"),
             )
         for lo in (0, 64):
             nc.vector.quantize_mx(

@@ -19,6 +19,7 @@ P = 128
 PACK = 4
 HEAD = 256
 QT = 256
+TAIL = 16
 X_CUTS = (0, 256, 512, 768, 1024)
 G_CUTS = (256, 512, 768, 1024)
 PASSES = ((0, 128), (128, 128), (256, 256), (512, 256), (768, 256))
@@ -41,6 +42,7 @@ def tile_picked_wroute2_lingelu_l_kernel(tc, x_words, x_scales, gate, w1, dst, o
         g_rest = keep.tile([P, T - HEAD], F32, name="g_rest")
         y_head = keep.tile([P, HEAD], F32, name="y_head")
         y_rest = keep.tile([P, T - HEAD], F32, name="y_rest")
+        y_tail = keep.tile([P, TAIL], F32, name="y_tail")
         window = keep.tile([P, U], F32, name="window")
 
         words = x_words[0].rearrange("p n t -> p (n t)")
@@ -89,8 +91,13 @@ def tile_picked_wroute2_lingelu_l_kernel(tc, x_words, x_scales, gate, w1, dst, o
                 start=True,
                 stop=True,
             )
-            nc.scalar.activation(y_t[:, a : a + n], acc[:], GELU)
+            if c + n < T:
+                nc.scalar.activation(y_t[:, a : a + n], acc[:], GELU)
+            else:
+                nc.scalar.activation(y_t[:, a : a + n - TAIL], acc[:, : n - TAIL], GELU)
+                nc.scalar.activation(y_tail[:], acc[:, n - TAIL :], GELU)
 
         nc.vector.tensor_tensor(window[:].indirect(offsets[:, : HEAD // 16]), y_head[:], g_head[:], MULT)
+        nc.vector.tensor_copy(out=y_rest[:, T - HEAD - TAIL :], in_=y_tail[:])
         nc.vector.tensor_tensor(window[:].indirect(offsets[:, HEAD // 16 :]), y_rest[:], g_rest[:], MULT)
         nc.sync.dma_start(out=out, in_=window[:])

@@ -20,9 +20,9 @@ PACK = 4
 HEAD = 256
 QT = 256
 TAIL = 16
-X_CUTS = (0, 256, 512, 768, 1024)
-G_CUTS = (256, 512, 768, 1024)
-PASSES = ((0, 128), (128, 128), (256, 256), (512, 256), (768, 256))
+X_CUTS = (0, 256, 768, 1024)
+G_CUTS = (256, 448, 640, 832, 1024)
+PASSES = ((0, 128), (128, 128), (256, 256), (512, 256), (768, 128), (896, 128))
 
 
 def tile_picked_wroute2_lingelu_l_kernel(tc, x_words, x_scales, gate, w1, dst, out):
@@ -58,10 +58,10 @@ def tile_picked_wroute2_lingelu_l_kernel(tc, x_words, x_scales, gate, w1, dst, o
                 out=x_plane[32 * q : 32 * q + 16, :].bitcast(I32),
                 in_=x_scales[0, 4 * q : 4 * q + 4, :].bitcast(I32).rearrange("r (c n) -> c r n", c=4),
             )
+        load_tokens(X_CUTS[1], X_CUTS[2])
         nc.sync.dma_start(out=g_head[:], in_=gate[:, :HEAD])
         nc.sync.dma_start(offsets[:], dst)
-        for lo, hi in zip(X_CUTS[1:-1], X_CUTS[2:]):
-            load_tokens(lo, hi)
+        load_tokens(X_CUTS[2], X_CUTS[3])
         for lo, hi in zip(G_CUTS[:-1], G_CUTS[1:]):
             nc.sync.dma_start(out=g_rest[:, lo - HEAD : hi - HEAD], in_=gate[:, lo:hi])
 

@@ -31,19 +31,19 @@ def tile_picked_wroute2_lingelu_l_kernel(tc, x_words, x_scales, gate, w1, dst, o
         keep = ctx.enter_context(tc.tile_pool(name="keep", bufs=1))
         psum = ctx.enter_context(tc.psum_pool(name="psum", bufs=1))
 
-        offsets = keep.tile([P, T // 16], U16, name="offsets")
-        w_pairs = [keep.tile([P, 2, N], F32, name="w_pair%d" % h) for h in range(2)]
+        offsets = keep.tile([P, T // 16], U16, name="offsets", align_bytes=256)
+        w_pairs = [keep.tile([P, 2, N], F32, name="w_pair%d" % h, align_bytes=256) for h in range(2)]
         w_grouped = keep.tile([P, N, PACK], BF16, name="w_grouped", align_bytes=64)
         w_codes = keep.tile([P, N], U32, name="w_codes", align_bytes=64)
         w_plane = keep.tile([P, N], U8, name="w_plane", align_bytes=64)
-        x_plane = keep.tile([P, QT], U8, name="x_plane", align_bytes=64)
-        x_codes = keep.tile([P, T], U32, name="x_codes", align_bytes=64)
-        g_head = keep.tile([P, HEAD], F32, name="g_head")
-        g_rest = keep.tile([P, T - HEAD], F32, name="g_rest")
+        x_plane = keep.tile([P, QT], U8, name="x_plane", align_bytes=256)
+        x_codes = keep.tile([P, T], U32, name="x_codes", align_bytes=256)
+        g_head = keep.tile([P, HEAD], F32, name="g_head", align_bytes=256)
+        g_rest = keep.tile([P, T - HEAD], F32, name="g_rest", align_bytes=256)
         y_head = keep.tile([P, HEAD], F32, name="y_head")
         y_rest = keep.tile([P, T - HEAD], F32, name="y_rest")
         y_tail = keep.tile([P, TAIL], F32, name="y_tail")
-        window = keep.tile([P, U], F32, name="window")
+        window = keep.tile([P, U], F32, name="window", align_bytes=256)
 
         words = x_words[0].rearrange("p n t -> p (n t)")
 

@@ -20,7 +20,8 @@ PACK = 4
 HEAD = 256
 QT = 256
 TAIL = 16
-X_CUTS = (0, 256, 768, 1024)
+X_CUTS = (0, 256, 768, 896, 1024)
+W_CUTS = (0, 64, 96, 128)
 G_CUTS = (256, 448, 640, 832, 1024)
 PASSES = ((0, 128), (128, 128), (256, 256), (512, 256), (768, 128), (896, 128))
 
@@ -32,7 +33,7 @@ def tile_picked_wroute2_lingelu_l_kernel(tc, x_words, x_scales, gate, w1, dst, o
         psum = ctx.enter_context(tc.psum_pool(name="psum", bufs=1))
 
         offsets = keep.tile([P, T // 16], U16, name="offsets", align_bytes=256)
-        w_pairs = [keep.tile([P, 2, N], F32, name="w_pair%d" % h, align_bytes=256) for h in range(2)]
+        w_rows = keep.tile([P, PACK, N], F32, name="w_rows", align_bytes=256)
         w_grouped = keep.tile([P, N, PACK], BF16, name="w_grouped", align_bytes=64)
         w_codes = keep.tile([P, N], U32, name="w_codes", align_bytes=64)
         w_plane = keep.tile([P, N], U8, name="w_plane", align_bytes=64)
@@ -50,33 +51,33 @@ def tile_picked_wroute2_lingelu_l_kernel(tc, x_words, x_scales, gate, w1, dst, o
         def load_tokens(lo, hi):
             nc.sync.dma_start(out=x_codes[:, lo:hi].bitcast(I32), in_=words[:, PACK * lo : PACK * hi].bitcast(I32))
 
-        for h in range(2):
-            nc.sync.dma_start(out=w_pairs[h][:], in_=w1.rearrange("(p j) n -> p j n", j=PACK)[:, 2 * h : 2 * h + 2, :])
+        nc.sync.dma_start(out=w_rows[:], in_=w1.rearrange("(p j) n -> p j n", j=PACK))
         load_tokens(X_CUTS[0], X_CUTS[1])
         for q in range(4):
             nc.sync.dma_start(
                 out=x_plane[32 * q : 32 * q + 16, :].bitcast(I32),
                 in_=x_scales[0, 4 * q : 4 * q + 4, :].bitcast(I32).rearrange("r (c n) -> c r n", c=4),
             )
-        load_tokens(X_CUTS[1], X_CUTS[2])
         nc.sync.dma_start(out=g_head[:], in_=gate[:, :HEAD])
+        load_tokens(X_CUTS[1], X_CUTS[2])
         nc.sync.dma_start(offsets[:], dst)
         load_tokens(X_CUTS[2], X_CUTS[3])
+        load_tokens(X_CUTS[3], X_CUTS[4])
         for lo, hi in zip(G_CUTS[:-1], G_CUTS[1:]):
             nc.sync.dma_start(out=g_rest[:, lo - HEAD : hi - HEAD], in_=gate[:, lo:hi])
 
         nc.vector.memset(window[:].bitcast(I32), 0)
 
-        for h, lo, hi in ((0, 0, 128), (1, 0, 64), (1, 64, 128)):
+        for lo, hi in zip(W_CUTS[:-1], W_CUTS[1:]):
             nc.vector.tensor_copy(
-                out=w_grouped[:, lo:hi, 2 * h : 2 * h + 2],
-                in_=w_pairs[h][:, :, lo:hi].rearrange("p t n -> p n t"),
+                out=w_grouped[:, lo:hi, :].rearrange("p (c i) t -> p c t i", i=2),
+                in_=w_rows[:, :, lo:hi].rearrange("p t (c i) -> p c t i", i=2),
             )
-        for lo in (0, 64):
+        for lo, hi in zip(W_CUTS[:-1], W_CUTS[1:]):
             nc.vector.quantize_mx(
-                out=w_codes[:, lo : lo + 64].bitcast(FP8X4),
-                scales=w_plane[:, lo : lo + 64],
-                in_=w_grouped[:, lo : lo + 64, :].rearrange("p n t -> p (n t)"),
+                out=w_codes[:, lo:hi].bitcast(FP8X4),
+                scales=w_plane[:, lo:hi],
+                in_=w_grouped[:, lo:hi, :].rearrange("p n t -> p (n t)"),
             )
 
         for i, (c, n) in enumerate(PASSES):

@@ -20,10 +20,10 @@ PACK = 4
 HEAD = 256
 QT = 256
 TAIL = 16
-X_CUTS = (0, 256, 768, 896, 1024)
+X_CUTS = (0, 384, 640, 896, 1024)
 W_CUTS = (0, 64, 96, 128)
 G_CUTS = (256, 448, 640, 832, 1024)
-PASSES = ((0, 128), (128, 128), (256, 256), (512, 256), (768, 128), (896, 128))
+PASSES = ((0, 128), (128, 128), (256, 128), (384, 128), (512, 128), (640, 128), (768, 128), (896, 128))
 
 
 def tile_picked_wroute2_lingelu_l_kernel(tc, x_words, x_scales, gate, w1, dst, out):
@@ -52,15 +52,16 @@ def tile_picked_wroute2_lingelu_l_kernel(tc, x_words, x_scales, gate, w1, dst, o
             nc.sync.dma_start(out=x_codes[:, lo:hi].bitcast(I32), in_=words[:, PACK * lo : PACK * hi].bitcast(I32))
 
         nc.sync.dma_start(out=w_rows[:], in_=w1.rearrange("(p j) n -> p j n", j=PACK))
-        load_tokens(X_CUTS[0], X_CUTS[1])
         for q in range(4):
+            if q == 2:
+                load_tokens(X_CUTS[0], X_CUTS[1])
             nc.sync.dma_start(
                 out=x_plane[32 * q : 32 * q + 16, :].bitcast(I32),
                 in_=x_scales[0, 4 * q : 4 * q + 4, :].bitcast(I32).rearrange("r (c n) -> c r n", c=4),
             )
         nc.sync.dma_start(out=g_head[:], in_=gate[:, :HEAD])
-        load_tokens(X_CUTS[1], X_CUTS[2])
         nc.sync.dma_start(offsets[:], dst)
+        load_tokens(X_CUTS[1], X_CUTS[2])
         load_tokens(X_CUTS[2], X_CUTS[3])
         load_tokens(X_CUTS[3], X_CUTS[4])
         for lo, hi in zip(G_CUTS[:-1], G_CUTS[1:]):

@@ -20,9 +20,9 @@ PACK = 4
 HEAD = 256
 QT = 256
 TAIL = 16
-X_CUTS = (0, 384, 640, 896, 1024)
+X_CUTS = (0, 512, 768, 896, 1024)
 W_CUTS = (0, 64, 96, 128)
-G_CUTS = (256, 448, 640, 832, 1024)
+G_CUTS = (0, 512, 640, 768, 896, 1024)
 PASSES = ((0, 128), (128, 128), (256, 128), (384, 128), (512, 128), (640, 128), (768, 128), (896, 128))
 
 
@@ -39,8 +39,7 @@ def tile_picked_wroute2_lingelu_l_kernel(tc, x_words, x_scales, gate, w1, dst, o
         w_plane = keep.tile([P, N], U8, name="w_plane", align_bytes=64)
         x_plane = keep.tile([P, QT], U8, name="x_plane", align_bytes=256)
         x_codes = keep.tile([P, T], U32, name="x_codes", align_bytes=256)
-        g_head = keep.tile([P, HEAD], F32, name="g_head", align_bytes=256)
-        g_rest = keep.tile([P, T - HEAD], F32, name="g_rest", align_bytes=256)
+        gates = keep.tile([P, T], F32, name="gates", align_bytes=256)
         y_head = keep.tile([P, HEAD], F32, name="y_head")
         y_rest = keep.tile([P, T - HEAD], F32, name="y_rest")
         y_tail = keep.tile([P, TAIL], F32, name="y_tail")
@@ -59,13 +58,12 @@ def tile_picked_wroute2_lingelu_l_kernel(tc, x_words, x_scales, gate, w1, dst, o
                 out=x_plane[32 * q : 32 * q + 16, :].bitcast(I32),
                 in_=x_scales[0, 4 * q : 4 * q + 4, :].bitcast(I32).rearrange("r (c n) -> c r n", c=4),
             )
-        nc.sync.dma_start(out=g_head[:], in_=gate[:, :HEAD])
         nc.sync.dma_start(offsets[:], dst)
-        load_tokens(X_CUTS[1], X_CUTS[2])
-        load_tokens(X_CUTS[2], X_CUTS[3])
-        load_tokens(X_CUTS[3], X_CUTS[4])
-        for lo, hi in zip(G_CUTS[:-1], G_CUTS[1:]):
-            nc.sync.dma_start(out=g_rest[:, lo - HEAD : hi - HEAD], in_=gate[:, lo:hi])
+        nc.sync.dma_start(out=gates[:, : G_CUTS[1]], in_=gate[:, : G_CUTS[1]])
+        for lo, hi in zip(X_CUTS[1:-1], X_CUTS[2:]):
+            load_tokens(lo, hi)
+        for lo, hi in zip(G_CUTS[1:-1], G_CUTS[2:]):
+            nc.sync.dma_start(out=gates[:, lo:hi], in_=gate[:, lo:hi])
 
         nc.vector.memset(window[:].bitcast(I32), 0)
 
@@ -99,7 +97,7 @@ def tile_picked_wroute2_lingelu_l_kernel(tc, x_words, x_scales, gate, w1, dst, o
                 nc.scalar.activation(y_t[:, a : a + n - TAIL], acc[:, : n - TAIL], GELU)
                 nc.scalar.activation(y_tail[:], acc[:, n - TAIL :], GELU)
 
-        nc.vector.tensor_tensor(window[:].indirect(offsets[:, : HEAD // 16]), y_head[:], g_head[:], MULT)
+        nc.vector.tensor_tensor(window[:].indirect(offsets[:, : HEAD // 16]), y_head[:], gates[:, :HEAD], MULT)
         nc.vector.tensor_copy(out=y_rest[:, T - HEAD - TAIL :], in_=y_tail[:])
-        nc.vector.tensor_tensor(window[:].indirect(offsets[:, HEAD // 16 :]), y_rest[:], g_rest[:], MULT)
+        nc.vector.tensor_tensor(window[:].indirect(offsets[:, HEAD // 16 :]), y_rest[:], gates[:, HEAD:], MULT)
         nc.sync.dma_start(out=out, in_=window[:])

@@ -13,17 +13,17 @@ U16 = mybir.dt.uint16
 U8 = mybir.dt.uint8
 FP8X4 = mybir.dt.float8_e4m3fn_x4
 GELU = mybir.ActivationFunctionType.Gelu_apprx_tanh
+COPY = mybir.ActivationFunctionType.Copy
 MULT = mybir.AluOpType.mult
+ADD = mybir.AluOpType.add
 
 P = 128
 PACK = 4
-HEAD = 256
 QT = 256
-TAIL = 16
-X_CUTS = (0, 512, 768, 896, 1024)
+PASS = 128
 W_CUTS = (0, 64, 96, 128)
-G_CUTS = (0, 512, 640, 768, 896, 1024)
-PASSES = ((0, 128), (128, 128), (256, 128), (384, 128), (512, 128), (640, 128), (768, 128), (896, 128))
+VECTOR_CLEARS = 256
+OUT_CUTS = (0, 256, 640, 1024, 1536, 2048)
 
 
 def tile_picked_wroute2_lingelu_l_kernel(tc, x_words, x_scales, gate, w1, dst, out):
@@ -40,32 +40,46 @@ def tile_picked_wroute2_lingelu_l_kernel(tc, x_words, x_scales, gate, w1, dst, o
         x_plane = keep.tile([P, QT], U8, name="x_plane", align_bytes=256)
         x_codes = keep.tile([P, T], U32, name="x_codes", align_bytes=256)
         gates = keep.tile([P, T], F32, name="gates", align_bytes=256)
-        y_head = keep.tile([P, HEAD], F32, name="y_head")
-        y_rest = keep.tile([P, T - HEAD], F32, name="y_rest")
-        y_tail = keep.tile([P, TAIL], F32, name="y_tail")
-        window = keep.tile([P, U], F32, name="window", align_bytes=256)
+        y = [keep.tile([P, QT], F32, name="y%d" % q) for q in range(4)]
+        gated = [keep.tile([P, QT], F32, name="gated%d" % h) for h in range(2)]
+        zero = keep.tile([P, 16], F32, name="zero")
+        by_vector = keep.tile([P, U], F32, name="by_vector", align_bytes=256)
+        by_scalar = keep.tile([P, U], F32, name="by_scalar", align_bytes=256)
 
         words = x_words[0].rearrange("p n t -> p (n t)")
 
         def load_tokens(lo, hi):
             nc.sync.dma_start(out=x_codes[:, lo:hi].bitcast(I32), in_=words[:, PACK * lo : PACK * hi].bitcast(I32))
 
-        nc.sync.dma_start(out=w_rows[:], in_=w1.rearrange("(p j) n -> p j n", j=PACK))
-        for q in range(4):
-            if q == 2:
-                load_tokens(X_CUTS[0], X_CUTS[1])
+        def load_scales(q):
             nc.sync.dma_start(
                 out=x_plane[32 * q : 32 * q + 16, :].bitcast(I32),
                 in_=x_scales[0, 4 * q : 4 * q + 4, :].bitcast(I32).rearrange("r (c n) -> c r n", c=4),
             )
-        nc.sync.dma_start(offsets[:], dst)
-        nc.sync.dma_start(out=gates[:, : G_CUTS[1]], in_=gate[:, : G_CUTS[1]])
-        for lo, hi in zip(X_CUTS[1:-1], X_CUTS[2:]):
-            load_tokens(lo, hi)
-        for lo, hi in zip(G_CUTS[1:-1], G_CUTS[2:]):
+
+        def load_gates(lo, hi):
             nc.sync.dma_start(out=gates[:, lo:hi], in_=gate[:, lo:hi])
 
-        nc.vector.memset(window[:].bitcast(I32), 0)
+        nc.sync.dma_start(out=w_rows[:], in_=w1.rearrange("(p j) n -> p j n", j=PACK))
+        load_scales(0)
+        load_scales(1)
+        load_tokens(0, 512)
+        load_scales(2)
+        load_scales(3)
+        load_tokens(512, 1024)
+        load_gates(0, 256)
+        load_gates(256, 512)
+        nc.sync.dma_start(offsets[:], dst)
+        load_gates(512, 1024)
+
+        nc.vector.memset(zero[:], 0.0)
+        nc.vector.memset(by_vector[:].bitcast(I32), 0)
+        nc.vector.memset(by_scalar[:, :VECTOR_CLEARS].bitcast(I32), 0)
+        nc.scalar.activation(
+            by_scalar[:, VECTOR_CLEARS:].rearrange("p (a b) -> p a b", b=16),
+            zero[:].unsqueeze(1).to_broadcast([P, (U - VECTOR_CLEARS) // 16, 16]),
+            GELU,
+        )
 
         for lo, hi in zip(W_CUTS[:-1], W_CUTS[1:]):
             nc.vector.tensor_copy(
@@ -79,25 +93,42 @@ def tile_picked_wroute2_lingelu_l_kernel(tc, x_words, x_scales, gate, w1, dst, o
                 in_=w_grouped[:, lo:hi, :].rearrange("p n t -> p (n t)"),
             )
 
-        for i, (c, n) in enumerate(PASSES):
-            y_t, a = (y_head, c) if c < HEAD else (y_rest, c - HEAD)
-            acc = psum.tile([P, n], F32, name="acc%d" % i)
+        def project(c):
+            q, a = divmod(c, QT)
+            acc = psum.tile([P, PASS], F32, name="acc%d" % (c // PASS))
             nc.tensor.matmul_mx(
                 out=acc[:],
                 lhsT=w_codes[:].bitcast(FP8X4),
                 lhsT_scale=w_plane[:],
-                rhs=x_codes[:, c : c + n].bitcast(FP8X4),
-                rhs_scale=x_plane[4 * (c // QT) :, c % QT : c % QT + n],
+                rhs=x_codes[:, c : c + PASS].bitcast(FP8X4),
+                rhs_scale=x_plane[4 * q :, a : a + PASS],
                 start=True,
                 stop=True,
             )
-            if c + n < T:
-                nc.scalar.activation(y_t[:, a : a + n], acc[:], GELU)
-            else:
-                nc.scalar.activation(y_t[:, a : a + n - TAIL], acc[:, : n - TAIL], GELU)
-                nc.scalar.activation(y_tail[:], acc[:, n - TAIL :], GELU)
+            nc.scalar.activation(y[q][:, a : a + PASS], acc[:], GELU)
 
-        nc.vector.tensor_tensor(window[:].indirect(offsets[:, : HEAD // 16]), y_head[:], gates[:, :HEAD], MULT)
-        nc.vector.tensor_copy(out=y_rest[:, T - HEAD - TAIL :], in_=y_tail[:])
-        nc.vector.tensor_tensor(window[:].indirect(offsets[:, HEAD // 16 :]), y_rest[:], gates[:, HEAD:], MULT)
-        nc.sync.dma_start(out=out, in_=window[:])
+        def entries(q):
+            return offsets[:, q * QT // 16 : (q + 1) * QT // 16]
+
+        def gate_values(q, lo, hi):
+            nc.vector.tensor_tensor(gated[q // 2][:, lo:hi], y[q][:, lo:hi], gates[:, q * QT + lo : q * QT + hi], MULT)
+
+        def scatter_vector(q):
+            nc.vector.tensor_tensor(by_vector[:].indirect(entries(q)), y[q][:], gates[:, q * QT : (q + 1) * QT], MULT)
+
+        def scatter_scalar(q):
+            nc.scalar.activation(by_scalar[:].indirect(entries(q)), gated[q // 2][:], COPY)
+
+        for c in range(0, T, PASS):
+            project(c)
+        gate_values(0, 0, 128)
+        gate_values(0, 128, 256)
+        scatter_vector(1)
+        scatter_scalar(0)
+        gate_values(2, 0, 256)
+        scatter_vector(3)
+        scatter_scalar(2)
+
+        for lo, hi in zip(OUT_CUTS[:-1], OUT_CUTS[1:]):
+            nc.vector.tensor_tensor(by_vector[:, lo:hi], by_vector[:, lo:hi], by_scalar[:, lo:hi], ADD)
+            nc.sync.dma_start(out=out[:, lo:hi], in_=by_vector[:, lo:hi])

@@ -20,7 +20,6 @@ ADD = mybir.AluOpType.add
 P = 128
 PACK = 4
 QT = 256
-PASS = 128
 W_CUTS = (0, 64, 96, 128)
 VECTOR_CLEARS = 256
 OUT_CUTS = (0, 256, 640, 1024, 1536, 2048)
@@ -41,10 +40,10 @@ def tile_picked_wroute2_lingelu_l_kernel(tc, x_words, x_scales, gate, w1, dst, o
         x_codes = keep.tile([P, T], U32, name="x_codes", align_bytes=256)
         gates = keep.tile([P, T], F32, name="gates", align_bytes=256)
         y = [keep.tile([P, QT], F32, name="y%d" % q) for q in range(4)]
-        gated = [keep.tile([P, QT], F32, name="gated%d" % h) for h in range(2)]
+        gated = [keep.tile([P, QT], F32, name="gated%d" % q) for q in range(4)]
         zero = keep.tile([P, 16], F32, name="zero")
-        by_vector = keep.tile([P, U], F32, name="by_vector", align_bytes=256)
-        by_scalar = keep.tile([P, U], F32, name="by_scalar", align_bytes=256)
+        first = keep.tile([P, U], F32, name="first", align_bytes=256)
+        second = keep.tile([P, U], F32, name="second", align_bytes=256)
 
         words = x_words[0].rearrange("p n t -> p (n t)")
 
@@ -67,16 +66,16 @@ def tile_picked_wroute2_lingelu_l_kernel(tc, x_words, x_scales, gate, w1, dst, o
         load_scales(2)
         load_scales(3)
         load_tokens(512, 1024)
-        load_gates(0, 256)
-        load_gates(256, 512)
+        load_gates(0, 512)
         nc.sync.dma_start(offsets[:], dst)
-        load_gates(512, 1024)
+        load_gates(512, 768)
+        load_gates(768, 1024)
 
         nc.vector.memset(zero[:], 0.0)
-        nc.vector.memset(by_vector[:].bitcast(I32), 0)
-        nc.vector.memset(by_scalar[:, :VECTOR_CLEARS].bitcast(I32), 0)
+        nc.vector.memset(first[:].bitcast(I32), 0)
+        nc.vector.memset(second[:, :VECTOR_CLEARS].bitcast(I32), 0)
         nc.scalar.activation(
-            by_scalar[:, VECTOR_CLEARS:].rearrange("p (a b) -> p a b", b=16),
+            second[:, VECTOR_CLEARS:].rearrange("p (a b) -> p a b", b=16),
             zero[:].unsqueeze(1).to_broadcast([P, (U - VECTOR_CLEARS) // 16, 16]),
             GELU,
         )
@@ -93,42 +92,49 @@ def tile_picked_wroute2_lingelu_l_kernel(tc, x_words, x_scales, gate, w1, dst, o
                 in_=w_grouped[:, lo:hi, :].rearrange("p n t -> p (n t)"),
             )
 
-        def project(c):
+        def project(c, width):
             q, a = divmod(c, QT)
-            acc = psum.tile([P, PASS], F32, name="acc%d" % (c // PASS))
+            acc = psum.tile([P, width], F32, name="acc%d" % c)
             nc.tensor.matmul_mx(
                 out=acc[:],
                 lhsT=w_codes[:].bitcast(FP8X4),
                 lhsT_scale=w_plane[:],
-                rhs=x_codes[:, c : c + PASS].bitcast(FP8X4),
-                rhs_scale=x_plane[4 * q :, a : a + PASS],
+                rhs=x_codes[:, c : c + width].bitcast(FP8X4),
+                rhs_scale=x_plane[4 * q :, a : a + width],
                 start=True,
                 stop=True,
             )
-            nc.scalar.activation(y[q][:, a : a + PASS], acc[:], GELU)
+            nc.scalar.activation(y[q][:, a : a + width], acc[:], GELU)
 
         def entries(q):
             return offsets[:, q * QT // 16 : (q + 1) * QT // 16]
 
         def gate_values(q, lo, hi):
-            nc.vector.tensor_tensor(gated[q // 2][:, lo:hi], y[q][:, lo:hi], gates[:, q * QT + lo : q * QT + hi], MULT)
+            nc.vector.tensor_tensor(gated[q][:, lo:hi], y[q][:, lo:hi], gates[:, q * QT + lo : q * QT + hi], MULT)
 
-        def scatter_vector(q):
-            nc.vector.tensor_tensor(by_vector[:].indirect(entries(q)), y[q][:], gates[:, q * QT : (q + 1) * QT], MULT)
+        def scatter_vector(q, window):
+            nc.vector.tensor_tensor(window[:].indirect(entries(q)), y[q][:], gates[:, q * QT : (q + 1) * QT], MULT)
 
-        def scatter_scalar(q):
-            nc.scalar.activation(by_scalar[:].indirect(entries(q)), gated[q // 2][:], COPY)
+        def scatter_scalar(q, window):
+            nc.scalar.activation(window[:].indirect(entries(q)), gated[q][:], COPY)
 
-        for c in range(0, T, PASS):
-            project(c)
+        project(0, 128)
+        project(128, 128)
+        project(256, 128)
+        project(384, 128)
+        project(512, 128)
+        project(640, 128)
+        project(768, 128)
+        project(896, 128)
         gate_values(0, 0, 128)
         gate_values(0, 128, 256)
-        scatter_vector(1)
-        scatter_scalar(0)
-        gate_values(2, 0, 256)
-        scatter_vector(3)
-        scatter_scalar(2)
+        gate_values(1, 0, 128)
+        gate_values(1, 128, 256)
+        scatter_vector(2, first)
+        scatter_scalar(0, second)
+        scatter_vector(3, first)
+        scatter_scalar(1, second)
 
         for lo, hi in zip(OUT_CUTS[:-1], OUT_CUTS[1:]):
-            nc.vector.tensor_tensor(by_vector[:, lo:hi], by_vector[:, lo:hi], by_scalar[:, lo:hi], ADD)
-            nc.sync.dma_start(out=out[:, lo:hi], in_=by_vector[:, lo:hi])
+            nc.vector.tensor_tensor(first[:, lo:hi], first[:, lo:hi], second[:, lo:hi], ADD)
+            nc.sync.dma_start(out=out[:, lo:hi], in_=first[:, lo:hi])

@@ -20,9 +20,7 @@ ADD = mybir.AluOpType.add
 P = 128
 PACK = 4
 QT = 256
-W_CUTS = (0, 64, 96, 128)
-VECTOR_CLEARS = 256
-OUT_CUTS = (0, 256, 640, 1024, 1536, 2048)
+OUT_CUTS = (0, 280, 624, 1032, 1504, 2048)
 
 
 def tile_picked_wroute2_lingelu_l_kernel(tc, x_words, x_scales, gate, w1, dst, out):
@@ -32,7 +30,7 @@ def tile_picked_wroute2_lingelu_l_kernel(tc, x_words, x_scales, gate, w1, dst, o
         psum = ctx.enter_context(tc.psum_pool(name="psum", bufs=1))
 
         offsets = keep.tile([P, T // 16], U16, name="offsets", align_bytes=256)
-        w_rows = keep.tile([P, PACK, N], F32, name="w_rows", align_bytes=256)
+        w_rows = keep.tile([P, PACK, N], F32, name="w_rows", tag="w_rows", align_bytes=256)
         w_grouped = keep.tile([P, N, PACK], BF16, name="w_grouped", align_bytes=64)
         w_codes = keep.tile([P, N], U32, name="w_codes", align_bytes=64)
         w_plane = keep.tile([P, N], U8, name="w_plane", align_bytes=64)
@@ -43,7 +41,6 @@ def tile_picked_wroute2_lingelu_l_kernel(tc, x_words, x_scales, gate, w1, dst, o
         gated = [keep.tile([P, QT], F32, name="gated%d" % q) for q in range(4)]
         zero = keep.tile([P, 16], F32, name="zero")
         first = keep.tile([P, U], F32, name="first", align_bytes=256)
-        second = keep.tile([P, U], F32, name="second", align_bytes=256)
 
         words = x_words[0].rearrange("p n t -> p (n t)")
 
@@ -66,31 +63,45 @@ def tile_picked_wroute2_lingelu_l_kernel(tc, x_words, x_scales, gate, w1, dst, o
         load_scales(2)
         load_scales(3)
         load_tokens(512, 1024)
-        load_gates(0, 512)
+        load_gates(0, 256)
+        load_gates(256, 512)
         nc.sync.dma_start(offsets[:], dst)
-        load_gates(512, 768)
-        load_gates(768, 1024)
+        load_gates(512, 1024)
 
-        nc.vector.memset(zero[:], 0.0)
-        nc.vector.memset(first[:].bitcast(I32), 0)
-        nc.vector.memset(second[:, :VECTOR_CLEARS].bitcast(I32), 0)
-        nc.scalar.activation(
-            second[:, VECTOR_CLEARS:].rearrange("p (a b) -> p a b", b=16),
-            zero[:].unsqueeze(1).to_broadcast([P, (U - VECTOR_CLEARS) // 16, 16]),
-            GELU,
-        )
-
-        for lo, hi in zip(W_CUTS[:-1], W_CUTS[1:]):
-            nc.vector.tensor_copy(
-                out=w_grouped[:, lo:hi, :].rearrange("p (c i) t -> p c t i", i=2),
-                in_=w_rows[:, :, lo:hi].rearrange("p t (c i) -> p c t i", i=2),
+        def clear_scalar(window, lo):
+            nc.scalar.activation(
+                window[:, lo:].rearrange("p (a b) -> p a b", b=16),
+                zero[:].unsqueeze(1).to_broadcast([P, (U - lo) // 16, 16]),
+                GELU,
             )
-        for lo, hi in zip(W_CUTS[:-1], W_CUTS[1:]):
+
+        def grouped(lo, hi):
+            return w_grouped[:, lo:hi, :].rearrange("p (c i) t -> p c t i", i=2)
+
+        def rows(lo, hi):
+            return w_rows[:, :, lo:hi].rearrange("p t (c i) -> p c t i", i=2)
+
+        def quantise(lo, hi):
             nc.vector.quantize_mx(
                 out=w_codes[:, lo:hi].bitcast(FP8X4),
                 scales=w_plane[:, lo:hi],
                 in_=w_grouped[:, lo:hi, :].rearrange("p n t -> p (n t)"),
             )
+
+        nc.vector.memset(zero[:], 0.0)
+        nc.vector.memset(first[:, : U - 64].bitcast(I32), 0)
+        clear_scalar(first, U - 64)
+
+        nc.vector.tensor_copy(out=grouped(64, 96), in_=rows(64, 96))
+        nc.vector.tensor_copy(out=grouped(0, 64), in_=rows(0, 64))
+        nc.scalar.copy(out=grouped(96, 128), in_=rows(96, 128))
+        quantise(64, 96)
+        quantise(96, 128)
+        quantise(0, 64)
+
+        second = keep.tile([P, U], F32, name="second", tag="w_rows", align_bytes=256)
+        nc.vector.memset(second[:, : U - 512].bitcast(I32), 0)
+        clear_scalar(second, U - 512)
 
         def project(c, width):
             q, a = divmod(c, QT)
@@ -128,12 +139,11 @@ def tile_picked_wroute2_lingelu_l_kernel(tc, x_words, x_scales, gate, w1, dst, o
         project(896, 128)
         gate_values(0, 0, 128)
         gate_values(0, 128, 256)
-        gate_values(1, 0, 128)
-        gate_values(1, 128, 256)
-        scatter_vector(2, first)
+        scatter_vector(1, first)
         scatter_scalar(0, second)
+        gate_values(2, 0, 256)
         scatter_vector(3, first)
-        scatter_scalar(1, second)
+        scatter_scalar(2, second)
 
         for lo, hi in zip(OUT_CUTS[:-1], OUT_CUTS[1:]):
             nc.vector.tensor_tensor(first[:, lo:hi], first[:, lo:hi], second[:, lo:hi], ADD)

@@ -20,7 +20,7 @@ ADD = mybir.AluOpType.add
 P = 128
 PACK = 4
 QT = 256
-OUT_CUTS = (0, 280, 624, 1032, 1504, 2048)
+OUT_CUTS = (0, 256, 640, 1024, 1536, 2048)
 
 
 def tile_picked_wroute2_lingelu_l_kernel(tc, x_words, x_scales, gate, w1, dst, out):

@@ -30,7 +30,6 @@ def tile_picked_wroute2_lingelu_l_kernel(tc, x_words, x_scales, gate, w1, dst, o
         psum = ctx.enter_context(tc.psum_pool(name="psum", bufs=1))
 
         offsets = keep.tile([P, T // 16], U16, name="offsets", align_bytes=256)
-        w_rows = keep.tile([P, PACK, N], F32, name="w_rows", tag="w_rows", align_bytes=256)
         w_grouped = keep.tile([P, N, PACK], BF16, name="w_grouped", align_bytes=64)
         w_codes = keep.tile([P, N], U32, name="w_codes", align_bytes=64)
         w_plane = keep.tile([P, N], U8, name="w_plane", align_bytes=64)
@@ -41,7 +40,9 @@ def tile_picked_wroute2_lingelu_l_kernel(tc, x_words, x_scales, gate, w1, dst, o
         gated = [keep.tile([P, QT], F32, name="gated%d" % q) for q in range(4)]
         zero = keep.tile([P, 16], F32, name="zero")
         first = keep.tile([P, U], F32, name="first", align_bytes=256)
+        second = keep.tile([P, U], F32, name="second", align_bytes=256)
 
+        w_rows = second[:, : PACK * N].rearrange("p (j n) -> p j n", j=PACK)
         words = x_words[0].rearrange("p n t -> p (n t)")
 
         def load_tokens(lo, hi):
@@ -56,7 +57,7 @@ def tile_picked_wroute2_lingelu_l_kernel(tc, x_words, x_scales, gate, w1, dst, o
         def load_gates(lo, hi):
             nc.sync.dma_start(out=gates[:, lo:hi], in_=gate[:, lo:hi])
 
-        nc.sync.dma_start(out=w_rows[:], in_=w1.rearrange("(p j) n -> p j n", j=PACK))
+        nc.sync.dma_start(out=w_rows, in_=w1.rearrange("(p j) n -> p j n", j=PACK))
         load_scales(0)
         load_scales(1)
         load_tokens(0, 512)
@@ -68,10 +69,10 @@ def tile_picked_wroute2_lingelu_l_kernel(tc, x_words, x_scales, gate, w1, dst, o
         nc.sync.dma_start(offsets[:], dst)
         load_gates(512, 1024)
 
-        def clear_scalar(window, lo):
+        def clear_scalar(lo, hi):
             nc.scalar.activation(
-                window[:, lo:].rearrange("p (a b) -> p a b", b=16),
-                zero[:].unsqueeze(1).to_broadcast([P, (U - lo) // 16, 16]),
+                second[:, lo:hi].rearrange("p (a b) -> p a b", b=16),
+                zero[:].unsqueeze(1).to_broadcast([P, (hi - lo) // 16, 16]),
                 GELU,
             )
 
@@ -89,8 +90,9 @@ def tile_picked_wroute2_lingelu_l_kernel(tc, x_words, x_scales, gate, w1, dst, o
             )
 
         nc.vector.memset(zero[:], 0.0)
-        nc.vector.memset(first[:, : U - 64].bitcast(I32), 0)
-        clear_scalar(first, U - 64)
+        nc.vector.memset(first[:].bitcast(I32), 0)
+        nc.vector.memset(second[:, PACK * N : U - 256].bitcast(I32), 0)
+        clear_scalar(U - 256, U)
 
         nc.vector.tensor_copy(out=grouped(64, 96), in_=rows(64, 96))
         nc.vector.tensor_copy(out=grouped(0, 64), in_=rows(0, 64))
@@ -99,9 +101,7 @@ def tile_picked_wroute2_lingelu_l_kernel(tc, x_words, x_scales, gate, w1, dst, o
         quantise(96, 128)
         quantise(0, 64)
 
-        second = keep.tile([P, U], F32, name="second", tag="w_rows", align_bytes=256)
-        nc.vector.memset(second[:, : U - 512].bitcast(I32), 0)
-        clear_scalar(second, U - 512)
+        nc.vector.memset(second[:, : PACK * N].bitcast(I32), 0)
 
         def project(c, width):
             q, a = divmod(c, QT)

@@ -20,6 +20,7 @@ ADD = mybir.AluOpType.add
 P = 128
 PACK = 4
 QT = 256
+EDGE = 64
 OUT_CUTS = (0, 256, 640, 1024, 1536, 2048)
 
 
@@ -41,7 +42,7 @@ def tile_picked_wroute2_lingelu_l_kernel(tc, x_words, x_scales, gate, w1, dst, o
         zero = keep.tile([P, 16], F32, name="zero")
         first = keep.tile([P, U], F32, name="first", align_bytes=256)
         second = keep.tile([P, U], F32, name="second", align_bytes=256)
-
+        edge = keep.tile([P, EDGE], F32, name="edge")
         w_rows = second[:, : PACK * N].rearrange("p (j n) -> p j n", j=PACK)
         words = x_words[0].rearrange("p n t -> p (n t)")
 
@@ -142,9 +143,13 @@ def tile_picked_wroute2_lingelu_l_kernel(tc, x_words, x_scales, gate, w1, dst, o
         scatter_vector(1, first)
         scatter_scalar(0, second)
         gate_values(2, 0, 256)
-        scatter_vector(3, first)
-        scatter_scalar(2, second)
+        scatter_scalar(2, first)
+        scatter_vector(3, second)
 
+        nc.vector.tensor_copy(out=edge[:], in_=first[:, U - EDGE :])
         for lo, hi in zip(OUT_CUTS[:-1], OUT_CUTS[1:]):
-            nc.vector.tensor_tensor(first[:, lo:hi], first[:, lo:hi], second[:, lo:hi], ADD)
+            inner = min(hi, U - EDGE)
+            nc.vector.tensor_tensor(first[:, lo:inner], first[:, lo:inner], second[:, lo:inner], ADD)
+            if hi > inner:
+                nc.vector.tensor_tensor(first[:, inner:hi], edge[:], second[:, inner:hi], ADD)
             nc.sync.dma_start(out=out[:, lo:hi], in_=first[:, lo:hi])

@@ -19,7 +19,14 @@ ADD = mybir.AluOpType.add
 
 P = 128
 PACK = 4
-QT = 256
+QUARTER = T // 4
+PASS = 128
+LIST_ROWS = 16
+STAGED = PACK * N
+
+W_SHORT, W_LONG, W_SCALAR = (64, 96), (0, 64), (96, 128)
+SCALAR_CLEARS = 256
+ZEROS = 16
 EDGE = 64
 OUT_CUTS = (0, 256, 640, 1024, 1536, 2048)
 
@@ -30,52 +37,54 @@ def tile_picked_wroute2_lingelu_l_kernel(tc, x_words, x_scales, gate, w1, dst, o
         keep = ctx.enter_context(tc.tile_pool(name="keep", bufs=1))
         psum = ctx.enter_context(tc.psum_pool(name="psum", bufs=1))
 
-        offsets = keep.tile([P, T // 16], U16, name="offsets", align_bytes=256)
+        offsets = keep.tile([P, T // LIST_ROWS], U16, name="offsets", align_bytes=256)
         w_grouped = keep.tile([P, N, PACK], BF16, name="w_grouped", align_bytes=64)
         w_codes = keep.tile([P, N], U32, name="w_codes", align_bytes=64)
         w_plane = keep.tile([P, N], U8, name="w_plane", align_bytes=64)
-        x_plane = keep.tile([P, QT], U8, name="x_plane", align_bytes=256)
+        x_plane = keep.tile([P, QUARTER], U8, name="x_plane", align_bytes=256)
         x_codes = keep.tile([P, T], U32, name="x_codes", align_bytes=256)
         gates = keep.tile([P, T], F32, name="gates", align_bytes=256)
-        y = [keep.tile([P, QT], F32, name="y%d" % q) for q in range(4)]
-        gated = [keep.tile([P, QT], F32, name="gated%d" % q) for q in range(4)]
-        zero = keep.tile([P, 16], F32, name="zero")
+        y = [keep.tile([P, QUARTER], F32, name="y%d" % q) for q in range(4)]
+        gated = {q: keep.tile([P, QUARTER], F32, name="gated%d" % q) for q in (0, 2)}
+        zero = keep.tile([P, ZEROS], F32, name="zero")
         first = keep.tile([P, U], F32, name="first", align_bytes=256)
         second = keep.tile([P, U], F32, name="second", align_bytes=256)
         edge = keep.tile([P, EDGE], F32, name="edge")
-        w_rows = second[:, : PACK * N].rearrange("p (j n) -> p j n", j=PACK)
+        w_rows = second[:, :STAGED].rearrange("p (t n) -> p t n", t=PACK)
         words = x_words[0].rearrange("p n t -> p (n t)")
 
         def load_tokens(lo, hi):
             nc.sync.dma_start(out=x_codes[:, lo:hi].bitcast(I32), in_=words[:, PACK * lo : PACK * hi].bitcast(I32))
 
-        def load_scales(q):
+        def load_scales(a):
             nc.sync.dma_start(
-                out=x_plane[32 * q : 32 * q + 16, :].bitcast(I32),
-                in_=x_scales[0, 4 * q : 4 * q + 4, :].bitcast(I32).rearrange("r (c n) -> c r n", c=4),
+                out=x_plane[32 * a : 32 * a + 16, :].bitcast(I32),
+                in_=x_scales[0, 4 * a : 4 * a + 4, :].bitcast(I32).rearrange("r (q n) -> q r n", q=4),
             )
 
         def load_gates(lo, hi):
             nc.sync.dma_start(out=gates[:, lo:hi], in_=gate[:, lo:hi])
 
-        nc.sync.dma_start(out=w_rows, in_=w1.rearrange("(p j) n -> p j n", j=PACK))
+        nc.sync.dma_start(out=w_rows, in_=w1.rearrange("(p t) n -> p t n", t=PACK))
         load_scales(0)
         load_scales(1)
-        load_tokens(0, 512)
+        load_tokens(0, T // 2)
         load_scales(2)
         load_scales(3)
-        load_tokens(512, 1024)
-        load_gates(0, 256)
-        load_gates(256, 512)
+        load_tokens(T // 2, T)
+        load_gates(0, QUARTER)
+        load_gates(QUARTER, 2 * QUARTER)
         nc.sync.dma_start(offsets[:], dst)
-        load_gates(512, 1024)
+        load_gates(2 * QUARTER, T)
 
-        def clear_scalar(lo, hi):
-            nc.scalar.activation(
-                second[:, lo:hi].rearrange("p (a b) -> p a b", b=16),
-                zero[:].unsqueeze(1).to_broadcast([P, (hi - lo) // 16, 16]),
-                GELU,
-            )
+        nc.vector.memset(zero[:], 0.0)
+        nc.vector.memset(first[:].bitcast(I32), 0)
+        nc.vector.memset(second[:, STAGED : U - SCALAR_CLEARS].bitcast(I32), 0)
+        nc.scalar.activation(
+            second[:, U - SCALAR_CLEARS :].rearrange("p (a b) -> p a b", b=ZEROS),
+            zero[:].unsqueeze(1).to_broadcast([P, SCALAR_CLEARS // ZEROS, ZEROS]),
+            GELU,
+        )
 
         def grouped(lo, hi):
             return w_grouped[:, lo:hi, :].rearrange("p (c i) t -> p c t i", i=2)
@@ -83,66 +92,53 @@ def tile_picked_wroute2_lingelu_l_kernel(tc, x_words, x_scales, gate, w1, dst, o
         def rows(lo, hi):
             return w_rows[:, :, lo:hi].rearrange("p t (c i) -> p c t i", i=2)
 
-        def quantise(lo, hi):
+        nc.vector.tensor_copy(out=grouped(*W_SHORT), in_=rows(*W_SHORT))
+        nc.vector.tensor_copy(out=grouped(*W_LONG), in_=rows(*W_LONG))
+        nc.scalar.copy(out=grouped(*W_SCALAR), in_=rows(*W_SCALAR))
+        for lo, hi in (W_SHORT, W_SCALAR, W_LONG):
             nc.vector.quantize_mx(
                 out=w_codes[:, lo:hi].bitcast(FP8X4),
                 scales=w_plane[:, lo:hi],
                 in_=w_grouped[:, lo:hi, :].rearrange("p n t -> p (n t)"),
             )
 
-        nc.vector.memset(zero[:], 0.0)
-        nc.vector.memset(first[:].bitcast(I32), 0)
-        nc.vector.memset(second[:, PACK * N : U - 256].bitcast(I32), 0)
-        clear_scalar(U - 256, U)
+        nc.vector.memset(second[:, :STAGED].bitcast(I32), 0)
 
-        nc.vector.tensor_copy(out=grouped(64, 96), in_=rows(64, 96))
-        nc.vector.tensor_copy(out=grouped(0, 64), in_=rows(0, 64))
-        nc.scalar.copy(out=grouped(96, 128), in_=rows(96, 128))
-        quantise(64, 96)
-        quantise(96, 128)
-        quantise(0, 64)
-
-        nc.vector.memset(second[:, : PACK * N].bitcast(I32), 0)
-
-        def project(c, width):
-            q, a = divmod(c, QT)
-            acc = psum.tile([P, width], F32, name="acc%d" % c)
+        for c in range(0, T, PASS):
+            q, lo = divmod(c, QUARTER)
+            acc = psum.tile([P, PASS], F32, name="acc%d" % c)
             nc.tensor.matmul_mx(
                 out=acc[:],
                 lhsT=w_codes[:].bitcast(FP8X4),
                 lhsT_scale=w_plane[:],
-                rhs=x_codes[:, c : c + width].bitcast(FP8X4),
-                rhs_scale=x_plane[4 * q :, a : a + width],
+                rhs=x_codes[:, c : c + PASS].bitcast(FP8X4),
+                rhs_scale=x_plane[4 * q :, lo : lo + PASS],
                 start=True,
                 stop=True,
             )
-            nc.scalar.activation(y[q][:, a : a + width], acc[:], GELU)
+            nc.scalar.activation(y[q][:, lo : lo + PASS], acc[:], GELU)
 
         def entries(q):
-            return offsets[:, q * QT // 16 : (q + 1) * QT // 16]
+            return offsets[:, q * QUARTER // LIST_ROWS : (q + 1) * QUARTER // LIST_ROWS]
 
         def gate_values(q, lo, hi):
-            nc.vector.tensor_tensor(gated[q][:, lo:hi], y[q][:, lo:hi], gates[:, q * QT + lo : q * QT + hi], MULT)
+            nc.vector.tensor_tensor(
+                gated[q][:, lo:hi], y[q][:, lo:hi], gates[:, q * QUARTER + lo : q * QUARTER + hi], MULT
+            )
 
         def scatter_vector(q, window):
-            nc.vector.tensor_tensor(window[:].indirect(entries(q)), y[q][:], gates[:, q * QT : (q + 1) * QT], MULT)
+            nc.vector.tensor_tensor(
+                window[:].indirect(entries(q)), y[q][:], gates[:, q * QUARTER : (q + 1) * QUARTER], MULT
+            )
 
         def scatter_scalar(q, window):
             nc.scalar.activation(window[:].indirect(entries(q)), gated[q][:], COPY)
 
-        project(0, 128)
-        project(128, 128)
-        project(256, 128)
-        project(384, 128)
-        project(512, 128)
-        project(640, 128)
-        project(768, 128)
-        project(896, 128)
-        gate_values(0, 0, 128)
-        gate_values(0, 128, 256)
+        gate_values(0, 0, PASS)
+        gate_values(0, PASS, QUARTER)
         scatter_vector(1, first)
         scatter_scalar(0, second)
-        gate_values(2, 0, 256)
+        gate_values(2, 0, QUARTER)
         scatter_scalar(2, first)
         scatter_vector(3, second)
 

@@ -24,6 +24,8 @@ PASS = 128
 LIST_ROWS = 16
 STAGED = PACK * N
 
+SPLIT = 544
+GATE_CUTS = (0, 256, 576, T)
 W_SHORT, W_LONG, W_SCALAR = (64, 96), (0, 64), (96, 128)
 SCALAR_CLEARS = 256
 ZEROS = 16
@@ -44,13 +46,14 @@ def tile_picked_wroute2_lingelu_l_kernel(tc, x_words, x_scales, gate, w1, dst, o
         x_plane = keep.tile([P, QUARTER], U8, name="x_plane", align_bytes=256)
         x_codes = keep.tile([P, T], U32, name="x_codes", align_bytes=256)
         gates = keep.tile([P, T], F32, name="gates", align_bytes=256)
-        y = [keep.tile([P, QUARTER], F32, name="y%d" % q) for q in range(4)]
-        gated = {q: keep.tile([P, QUARTER], F32, name="gated%d" % q) for q in (0, 2)}
+        y = keep.tile([P, T], F32, name="y")
+        gated = keep.tile([P, SPLIT], F32, name="gated")
         zero = keep.tile([P, ZEROS], F32, name="zero")
-        first = keep.tile([P, U], F32, name="first", align_bytes=256)
-        second = keep.tile([P, U], F32, name="second", align_bytes=256)
+        one = keep.tile([P, 1], F32, name="one")
+        by_vector = keep.tile([P, U], F32, name="by_vector", align_bytes=256)
+        by_scalar = keep.tile([P, U], F32, name="by_scalar", align_bytes=256)
         edge = keep.tile([P, EDGE], F32, name="edge")
-        w_rows = second[:, :STAGED].rearrange("p (t n) -> p t n", t=PACK)
+        w_rows = by_scalar[:, :STAGED].rearrange("p (t n) -> p t n", t=PACK)
         words = x_words[0].rearrange("p n t -> p (n t)")
 
         def load_tokens(lo, hi):
@@ -62,7 +65,8 @@ def tile_picked_wroute2_lingelu_l_kernel(tc, x_words, x_scales, gate, w1, dst, o
                 in_=x_scales[0, 4 * a : 4 * a + 4, :].bitcast(I32).rearrange("r (q n) -> q r n", q=4),
             )
 
-        def load_gates(lo, hi):
+        def load_gates(piece):
+            lo, hi = GATE_CUTS[piece], GATE_CUTS[piece + 1]
             nc.sync.dma_start(out=gates[:, lo:hi], in_=gate[:, lo:hi])
 
         nc.sync.dma_start(out=w_rows, in_=w1.rearrange("(p t) n -> p t n", t=PACK))
@@ -72,16 +76,17 @@ def tile_picked_wroute2_lingelu_l_kernel(tc, x_words, x_scales, gate, w1, dst, o
         load_scales(2)
         load_scales(3)
         load_tokens(T // 2, T)
-        load_gates(0, QUARTER)
-        load_gates(QUARTER, 2 * QUARTER)
+        load_gates(0)
+        load_gates(1)
         nc.sync.dma_start(offsets[:], dst)
-        load_gates(2 * QUARTER, T)
+        load_gates(2)
 
         nc.vector.memset(zero[:], 0.0)
-        nc.vector.memset(first[:].bitcast(I32), 0)
-        nc.vector.memset(second[:, STAGED : U - SCALAR_CLEARS].bitcast(I32), 0)
+        nc.vector.memset(one[:], 1.0)
+        nc.vector.memset(by_vector[:].bitcast(I32), 0)
+        nc.vector.memset(by_scalar[:, STAGED : U - SCALAR_CLEARS].bitcast(I32), 0)
         nc.scalar.activation(
-            second[:, U - SCALAR_CLEARS :].rearrange("p (a b) -> p a b", b=ZEROS),
+            by_scalar[:, U - SCALAR_CLEARS :].rearrange("p (a b) -> p a b", b=ZEROS),
             zero[:].unsqueeze(1).to_broadcast([P, SCALAR_CLEARS // ZEROS, ZEROS]),
             GELU,
         )
@@ -102,7 +107,7 @@ def tile_picked_wroute2_lingelu_l_kernel(tc, x_words, x_scales, gate, w1, dst, o
                 in_=w_grouped[:, lo:hi, :].rearrange("p n t -> p (n t)"),
             )
 
-        nc.vector.memset(second[:, :STAGED].bitcast(I32), 0)
+        nc.vector.memset(by_scalar[:, :STAGED].bitcast(I32), 0)
 
         for c in range(0, T, PASS):
             q, lo = divmod(c, QUARTER)
@@ -116,36 +121,19 @@ def tile_picked_wroute2_lingelu_l_kernel(tc, x_words, x_scales, gate, w1, dst, o
                 start=True,
                 stop=True,
             )
-            nc.scalar.activation(y[q][:, lo : lo + PASS], acc[:], GELU)
+            nc.scalar.activation(y[:, c : c + PASS], acc[:], GELU)
+            if c < SPLIT:
+                hi = min(c + PASS, SPLIT)
+                nc.vector.tensor_tensor(gated[:, c:hi], y[:, c:hi], gates[:, c:hi], MULT)
 
-        def entries(q):
-            return offsets[:, q * QUARTER // LIST_ROWS : (q + 1) * QUARTER // LIST_ROWS]
+        cut = SPLIT // LIST_ROWS
+        nc.scalar.activation(by_scalar[:].indirect(offsets[:, :cut]), gated[:], COPY, scale=one[:])
+        nc.vector.tensor_tensor(by_vector[:].indirect(offsets[:, cut:]), y[:, SPLIT:], gates[:, SPLIT:], MULT)
 
-        def gate_values(q, lo, hi):
-            nc.vector.tensor_tensor(
-                gated[q][:, lo:hi], y[q][:, lo:hi], gates[:, q * QUARTER + lo : q * QUARTER + hi], MULT
-            )
-
-        def scatter_vector(q, window):
-            nc.vector.tensor_tensor(
-                window[:].indirect(entries(q)), y[q][:], gates[:, q * QUARTER : (q + 1) * QUARTER], MULT
-            )
-
-        def scatter_scalar(q, window):
-            nc.scalar.activation(window[:].indirect(entries(q)), gated[q][:], COPY)
-
-        gate_values(0, 0, PASS)
-        gate_values(0, PASS, QUARTER)
-        scatter_vector(1, first)
-        scatter_scalar(0, second)
-        gate_values(2, 0, QUARTER)
-        scatter_scalar(2, first)
-        scatter_vector(3, second)
-
-        nc.vector.tensor_copy(out=edge[:], in_=first[:, U - EDGE :])
+        nc.vector.tensor_copy(out=edge[:], in_=by_vector[:, U - EDGE :])
         for lo, hi in zip(OUT_CUTS[:-1], OUT_CUTS[1:]):
             inner = min(hi, U - EDGE)
-            nc.vector.tensor_tensor(first[:, lo:inner], first[:, lo:inner], second[:, lo:inner], ADD)
+            nc.vector.tensor_tensor(by_vector[:, lo:inner], by_vector[:, lo:inner], by_scalar[:, lo:inner], ADD)
             if hi > inner:
-                nc.vector.tensor_tensor(first[:, inner:hi], edge[:], second[:, inner:hi], ADD)
-            nc.sync.dma_start(out=out[:, lo:hi], in_=first[:, lo:hi])
+                nc.vector.tensor_tensor(by_vector[:, inner:hi], edge[:], by_scalar[:, inner:hi], ADD)
+            nc.sync.dma_start(out=out[:, lo:hi], in_=by_vector[:, lo:hi])

@@ -24,8 +24,8 @@ PASS = 128
 LIST_ROWS = 16
 STAGED = PACK * N
 
-SPLIT = 544
-GATE_CUTS = (0, 256, 576, T)
+SPLIT = 512
+GATE_CUTS = (0, 256, 512, T)
 W_SHORT, W_LONG, W_SCALAR = (64, 96), (0, 64), (96, 128)
 SCALAR_CLEARS = 256
 ZEROS = 16

@@ -130,10 +130,10 @@ def tile_picked_wroute2_lingelu_l_kernel(tc, x_words, x_scales, gate, w1, dst, o
         nc.scalar.activation(by_scalar[:].indirect(offsets[:, :cut]), gated[:], COPY, scale=one[:])
         nc.vector.tensor_tensor(by_vector[:].indirect(offsets[:, cut:]), y[:, SPLIT:], gates[:, SPLIT:], MULT)
 
-        nc.vector.tensor_copy(out=edge[:], in_=by_vector[:, U - EDGE :])
+        nc.vector.tensor_copy(out=edge[:], in_=by_scalar[:, U - EDGE :])
         for lo, hi in zip(OUT_CUTS[:-1], OUT_CUTS[1:]):
             inner = min(hi, U - EDGE)
-            nc.vector.tensor_tensor(by_vector[:, lo:inner], by_vector[:, lo:inner], by_scalar[:, lo:inner], ADD)
+            nc.vector.tensor_tensor(by_scalar[:, lo:inner], by_scalar[:, lo:inner], by_vector[:, lo:inner], ADD)
             if hi > inner:
-                nc.vector.tensor_tensor(by_vector[:, inner:hi], edge[:], by_scalar[:, inner:hi], ADD)
-            nc.sync.dma_start(out=out[:, lo:hi], in_=by_vector[:, lo:hi])
+                nc.vector.tensor_tensor(by_scalar[:, inner:hi], edge[:], by_vector[:, inner:hi], ADD)
+            nc.sync.dma_start(out=out[:, lo:hi], in_=by_scalar[:, lo:hi])

from contextlib import ExitStack

import concourse.mybir as mybir

K, T, N, U = 512, 1024, 128, 2048
FLOPS = 2 * K * T * N

F32 = mybir.dt.float32
BF16 = mybir.dt.bfloat16
I32 = mybir.dt.int32
U32 = mybir.dt.uint32
U16 = mybir.dt.uint16
U8 = mybir.dt.uint8
FP8X4 = mybir.dt.float8_e4m3fn_x4
GELU = mybir.ActivationFunctionType.Gelu_apprx_tanh
COPY = mybir.ActivationFunctionType.Copy
MULT = mybir.AluOpType.mult
ADD = mybir.AluOpType.add

P = 128
PACK = 4
QUARTER = T // 4
PASS = 128
LIST_ROWS = 16
STAGED = PACK * N

SPLIT = 512
GATE_CUTS = (0, 256, 512, T)
W_SHORT, W_LONG, W_SCALAR = (64, 96), (0, 64), (96, 128)
SCALAR_CLEARS = 256
ZEROS = 16
EDGE = 64
OUT_CUTS = (0, 256, 640, 1024, 1536, 2048)


def tile_picked_wroute2_lingelu_l_kernel(tc, x_words, x_scales, gate, w1, dst, out):
    nc = tc.nc
    with ExitStack() as ctx:
        keep = ctx.enter_context(tc.tile_pool(name="keep", bufs=1))
        psum = ctx.enter_context(tc.psum_pool(name="psum", bufs=1))

        offsets = keep.tile([P, T // LIST_ROWS], U16, name="offsets", align_bytes=256)
        w_grouped = keep.tile([P, N, PACK], BF16, name="w_grouped", align_bytes=64)
        w_codes = keep.tile([P, N], U32, name="w_codes", align_bytes=64)
        w_plane = keep.tile([P, N], U8, name="w_plane", align_bytes=64)
        x_plane = keep.tile([P, QUARTER], U8, name="x_plane", align_bytes=256)
        x_codes = keep.tile([P, T], U32, name="x_codes", align_bytes=256)
        gates = keep.tile([P, T], F32, name="gates", align_bytes=256)
        y = keep.tile([P, T], F32, name="y")
        gated = keep.tile([P, SPLIT], F32, name="gated")
        zero = keep.tile([P, ZEROS], F32, name="zero")
        one = keep.tile([P, 1], F32, name="one")
        by_vector = keep.tile([P, U], F32, name="by_vector", align_bytes=256)
        by_scalar = keep.tile([P, U], F32, name="by_scalar", align_bytes=256)
        edge = keep.tile([P, EDGE], F32, name="edge")
        w_rows = by_scalar[:, :STAGED].rearrange("p (t n) -> p t n", t=PACK)
        words = x_words[0].rearrange("p n t -> p (n t)")

        def load_tokens(lo, hi):
            nc.sync.dma_start(out=x_codes[:, lo:hi].bitcast(I32), in_=words[:, PACK * lo : PACK * hi].bitcast(I32))

        def load_scales(a):
            nc.sync.dma_start(
                out=x_plane[32 * a : 32 * a + 16, :].bitcast(I32),
                in_=x_scales[0, 4 * a : 4 * a + 4, :].bitcast(I32).rearrange("r (q n) -> q r n", q=4),
            )

        def load_gates(piece):
            lo, hi = GATE_CUTS[piece], GATE_CUTS[piece + 1]
            nc.sync.dma_start(out=gates[:, lo:hi], in_=gate[:, lo:hi])

        nc.sync.dma_start(out=w_rows, in_=w1.rearrange("(p t) n -> p t n", t=PACK))
        load_scales(0)
        load_scales(1)
        load_tokens(0, T // 2)
        load_scales(2)
        load_scales(3)
        load_tokens(T // 2, T)
        load_gates(0)
        load_gates(1)
        nc.sync.dma_start(offsets[:], dst)
        load_gates(2)

        nc.vector.memset(zero[:], 0.0)
        nc.vector.memset(one[:], 1.0)
        nc.vector.memset(by_vector[:].bitcast(I32), 0)
        nc.vector.memset(by_scalar[:, STAGED : U - SCALAR_CLEARS].bitcast(I32), 0)
        nc.scalar.activation(
            by_scalar[:, U - SCALAR_CLEARS :].rearrange("p (a b) -> p a b", b=ZEROS),
            zero[:].unsqueeze(1).to_broadcast([P, SCALAR_CLEARS // ZEROS, ZEROS]),
            GELU,
        )

        def grouped(lo, hi):
            return w_grouped[:, lo:hi, :].rearrange("p (c i) t -> p c t i", i=2)

        def rows(lo, hi):
            return w_rows[:, :, lo:hi].rearrange("p t (c i) -> p c t i", i=2)

        nc.vector.tensor_copy(out=grouped(*W_SHORT), in_=rows(*W_SHORT))
        nc.vector.tensor_copy(out=grouped(*W_LONG), in_=rows(*W_LONG))
        nc.scalar.copy(out=grouped(*W_SCALAR), in_=rows(*W_SCALAR))
        for lo, hi in (W_SHORT, W_SCALAR, W_LONG):
            nc.vector.quantize_mx(
                out=w_codes[:, lo:hi].bitcast(FP8X4),
                scales=w_plane[:, lo:hi],
                in_=w_grouped[:, lo:hi, :].rearrange("p n t -> p (n t)"),
            )

        nc.vector.memset(by_scalar[:, :STAGED].bitcast(I32), 0)

        for c in range(0, T, PASS):
            q, lo = divmod(c, QUARTER)
            acc = psum.tile([P, PASS], F32, name="acc%d" % c)
            nc.tensor.matmul_mx(
                out=acc[:],
                lhsT=w_codes[:].bitcast(FP8X4),
                lhsT_scale=w_plane[:],
                rhs=x_codes[:, c : c + PASS].bitcast(FP8X4),
                rhs_scale=x_plane[4 * q :, lo : lo + PASS],
                start=True,
                stop=True,
            )
            nc.scalar.activation(y[:, c : c + PASS], acc[:], GELU)
            if c < SPLIT:
                hi = min(c + PASS, SPLIT)
                nc.vector.tensor_tensor(gated[:, c:hi], y[:, c:hi], gates[:, c:hi], MULT)

        cut = SPLIT // LIST_ROWS
        nc.scalar.activation(by_scalar[:].indirect(offsets[:, :cut]), gated[:], COPY, scale=one[:])
        nc.vector.tensor_tensor(by_vector[:].indirect(offsets[:, cut:]), y[:, SPLIT:], gates[:, SPLIT:], MULT)

        nc.vector.tensor_copy(out=edge[:], in_=by_scalar[:, U - EDGE :])
        for lo, hi in zip(OUT_CUTS[:-1], OUT_CUTS[1:]):
            inner = min(hi, U - EDGE)
            nc.vector.tensor_tensor(by_scalar[:, lo:inner], by_scalar[:, lo:inner], by_vector[:, lo:inner], ADD)
            if hi > inner:
                nc.vector.tensor_tensor(by_scalar[:, inner:hi], edge[:], by_vector[:, inner:hi], ADD)
            nc.sync.dma_start(out=out[:, lo:hi], in_=by_scalar[:, lo:hi])
